import numpy as np
import ml_dtypes


def mxq(x, axis, fmt="e4m3"):
    dtype, down = {"e4m3": (ml_dtypes.float8_e4m3fn, 7), "e5m2": (ml_dtypes.float8_e5m2, 14)}[fmt]
    v = np.moveaxis(np.asarray(x, np.float32).astype(ml_dtypes.bfloat16).astype(np.float64), axis, -1)
    blocks = v.reshape(v.shape[:-1] + (-1, 32))
    amax = np.abs(blocks).max(-1, keepdims=True)
    byte = np.maximum(np.where(amax > 0, np.frexp(amax)[1] - 1 + 127, 0) - down, 1)
    scale = np.exp2(byte - 127.0)
    codes = (blocks / scale).astype(np.float32).astype(dtype).astype(np.float64)
    return np.moveaxis((codes * scale).reshape(v.shape), -1, axis)


WIDE = False


def mx_kscale(k):
    if not WIDE:
        return np.ones(k)
    levels = np.array([10, -10, 5, -5, 0])
    if k % 512:
        return np.exp2(np.random.permutation(np.resize(levels, k // 32))).repeat(32)
    a = np.empty((k // 512, 16))
    for p in range(k // 512):
        a[p, :8] = np.random.permutation(np.resize(levels, 8))
        for g in range(8):
            far = levels[np.abs(levels - a[p, g]) >= 10]
            a[p, g + 8] = far[np.random.randint(len(far))]
    return np.exp2(a.ravel()).repeat(32)


def f64(x):
    return np.asarray(x).astype(np.float64)


def striped(idx):
    return np.tile(idx.reshape(-1, 16).T, (8, 1)).astype(np.uint16)


def unstriped(offs):
    return offs[:16].T.reshape(-1).astype(np.int64)


E2M1 = np.array([0.0, 0.5, 1.0, 1.5, 2.0, 3.0, 4.0, 6.0, -0.0, -0.5, -1.0, -1.5, -2.0, -3.0, -4.0, -6.0])


def pack_weight(w, fmt):
    k, n = w.shape
    w = f64(np.asarray(w, np.float32).astype(ml_dtypes.bfloat16)).reshape(k // 32, 32, n)
    amax = np.abs(w).max(1)
    if fmt == "e4m3":
        byte = np.frexp(amax)[1] - 1 + 127 - 7
    else:
        mant, ex = np.frexp(amax / 6.0)
        byte = np.where(mant > 0.5, ex, ex - 1) + 127
    byte = np.clip(np.where(amax > 0, byte, 1), 1, 254)
    scaled = (w * np.exp2(127.0 - byte)[:, None, :]).reshape(k, n).astype(np.float32)
    by_word = np.ascontiguousarray(scaled.reshape(k // 512, 128, 4, n).transpose(0, 1, 3, 2))
    if fmt == "e4m3":
        words = by_word.astype(ml_dtypes.float8_e4m3fn).view(np.uint8)
    else:
        c = by_word.astype(ml_dtypes.float4_e2m1fn).view(np.uint8) & 0xF
        words = (c[..., 0::2] | (c[..., 1::2] << 4)).reshape(k // 512, 128, 2 * n)
    return np.ascontiguousarray(words), np.ascontiguousarray(byte.astype(np.uint8).reshape(k // 512, 16, n))


def unpack_weight(words, scales, fmt):
    g, _, n = scales.shape
    words = np.ascontiguousarray(words).reshape(g, 128, n, -1)
    if fmt == "e4m3":
        vals = words.view(ml_dtypes.float8_e4m3fn).astype(np.float64)
    else:
        nib = np.empty((g, 128, n, 4), np.uint8)
        nib[..., 0::2] = words & 0xF
        nib[..., 1::2] = words >> 4
        vals = E2M1[nib]
    vals = vals * np.repeat(np.exp2(scales.astype(np.float64) - 127.0), 8, axis=1)[..., None]
    return vals.transpose(0, 1, 3, 2).reshape(g * 512, n)


def gelu(v):
    return 0.5 * v * (1.0 + np.tanh(np.sqrt(2.0 / np.pi) * (v + 0.044715 * v**3)))


K, H, N, T, S, T2, P = 1536, 512, 768, 2048, 1024, 2048, 1024


def setup_inputs():
    n = np.random.standard_normal
    s = mx_kscale(K)[:, None]
    u = mx_kscale(H)[:, None]
    tab_words, tab_scales = pack_weight(n((K, T)) * s, "e4m3")
    wk_words, wk_scales = pack_weight(n((K, H)) * 2.3 / np.sqrt(K) / s, "e2m1")
    return {
        "tab_words": tab_words, "tab_scales": tab_scales,
        "offs": striped(np.random.permutation(T)[:S]),
        "offs2": striped(np.random.permutation(T2)[:S]),
        "offs3": striped(np.random.permutation(T2)[:P]),
        "wk_words": wk_words, "wk_scales": wk_scales,
        "bk": n(H).astype(np.float32),
        "wn": (n((K, H)) * 0.8 / np.sqrt(K) / s * u.T).astype(np.float32),
        "page0": (n((H, T2)) * 1.2 * u).astype(np.float32),
        "w3": (n((H, N)) * 1.5 / np.sqrt(H) / u).astype(np.float32),
        "gain": np.exp(0.5 * n(N)).astype(np.float32),
    }


def reference(tab_words, tab_scales, offs, offs2, offs3, wk_words, wk_scales, bk, wn, page0, w3, gain):
    v = unpack_weight(tab_words, tab_scales, "e4m3")[:, unstriped(offs)]
    wk = unpack_weight(wk_words, wk_scales, "e2m1")
    keep = 1.0 / (1.0 + np.exp(-((wk.T @ v) + f64(bk)[:, None])))
    fresh = mxq(f64(wn), 0, "e4m3").T @ v
    page = f64(page0).copy()
    l2 = unstriped(offs2)
    page[:, l2] = np.maximum(page[:, l2] * keep, fresh)
    x = mxq(page[:, unstriped(offs3)], 0, "e4m3")
    y = mxq(f64(w3), 0, "e4m3").T @ x
    return f64(gain)[:, None] * np.tanh(y)

@@ -1,0 +1,291 @@
+from contextlib import ExitStack
+
+import concourse.mybir as mybir
+
+K, H, N, T, S, T2, P3 = 1536, 512, 768, 2048, 1024, 2048, 1024
+FLOPS = 2 * (2 * K * H * S + H * N * P3)
+
+F32 = mybir.dt.float32
+BF16 = mybir.dt.bfloat16
+I32 = mybir.dt.int32
+U32 = mybir.dt.uint32
+U16 = mybir.dt.uint16
+U8 = mybir.dt.uint8
+FP8X4 = mybir.dt.float8_e4m3fn_x4
+FP4X4 = mybir.dt.float4_e2m1fn_x4
+ACT = mybir.ActivationFunctionType
+ALU = mybir.AluOpType
+
+P = 128
+PACK = 4
+PASSES = K // (P * PACK)
+BANK = 512
+HALVES = S // BANK
+N_TILES = N // P
+CHUNKS = (256, 256, 256, 256)
+PLANE_ROWS = 100
+
+
+def tile_list_hinge_history_update_kernel(
+    tc, tab_words, tab_scales, offs, offs2, offs3, wk_words, wk_scales, bk, wn, page0, w3, gain, out
+):
+    nc = tc.nc
+    with ExitStack() as ctx:
+        lists = ctx.enter_context(tc.tile_pool(name="lists", bufs=1))
+        held = ctx.enter_context(tc.tile_pool(name="held", bufs=1))
+        ring = ctx.enter_context(tc.tile_pool(name="ring", bufs=2))
+        psum = ctx.enter_context(tc.psum_pool(name="psum", bufs=1))
+
+        idx = lists.tile([P, S // 16], U16, name="idx")
+        idx2 = lists.tile([P, S // 16], U16, name="idx2")
+        idx3 = lists.tile([P, P3 // 16], U16, name="idx3")
+
+        tab_sc = held.tile([P, T], U8, name="tab_sc", align_bytes=64)
+        wk_sc_raw = held.tile([P, PASSES, H], U8, name="wk_sc_raw", align_bytes=64)
+        v_sc_moved = [held.tile([P, S], U8, name="v_sc_moved%d" % a, align_bytes=64) for a in range(1, PASSES)]
+        nc.vector.memset(tab_sc[:].bitcast(I32), 0)
+        nc.vector.memset(wk_sc_raw[:].rearrange("p a n -> p (a n)").bitcast(I32), 0)
+        for moved in v_sc_moved:
+            nc.vector.memset(moved[:].bitcast(I32), 0)
+
+        for q in range(4):
+            nc.scalar.dma_start(
+                out=tab_sc[32 * q : 32 * q + 4 * PASSES, :].bitcast(I32),
+                in_=tab_scales[:, 4 * q : 4 * q + 4, :].bitcast(I32),
+            )
+        for q in range(4):
+            nc.gpsimd.dma_start(
+                out=wk_sc_raw[32 * q : 32 * q + 4, :, :].bitcast(I32),
+                in_=wk_scales[:, 4 * q : 4 * q + 4, :].rearrange("a r n -> r a n").bitcast(I32),
+            )
+        bias = held.tile([P, PACK], F32, name="bias")
+        nc.gpsimd.dma_start(out=bias[:], in_=bk.rearrange("(p t) -> p t", t=PACK))
+        gains = held.tile([P, N_TILES], F32, name="gains")
+
+        tab_w = [held.tile([P, T], I32, name="tab_w%d" % a, align_bytes=64) for a in range(PASSES)]
+        wk_raw = held.tile([P, PASSES, H // 2], I32, name="wk_raw", align_bytes=64)
+        page = [held.tile([P, T2], F32, name="page%d" % t, align_bytes=64) for t in range(PACK)]
+        wn_raw = [held.tile([P, PACK, H], F32, name="wn_raw%d" % a, align_bytes=64) for a in range(PASSES)]
+        w3_raw = held.tile([P, PACK, N], F32, name="w3_raw", align_bytes=64)
+        page_rows = page0.rearrange("(p t) c -> t p c", t=PACK)
+
+        def load_table(a):
+            nc.sync.dma_start(out=tab_w[a][:], in_=tab_words[a].rearrange("p n i -> p (n i)").bitcast(I32))
+
+        def load_wn(a):
+            rows = wn[a * P * PACK : (a + 1) * P * PACK, :]
+            nc.sync.dma_start(out=wn_raw[a][:], in_=rows.rearrange("(p j) c -> p j c", j=PACK))
+
+        nc.sync.dma_start(idx[:], offs)
+        load_table(0)
+        nc.sync.dma_start(out=wk_raw[:], in_=wk_words.rearrange("a p n -> p a n").bitcast(I32))
+        load_table(1)
+        load_table(2)
+        nc.sync.dma_start(idx2[:], offs2)
+        nc.sync.dma_start(out=page[0][:], in_=page_rows[0])
+        for a in range(PASSES):
+            load_wn(a)
+        nc.sync.dma_start(out=page[1][:], in_=page_rows[1])
+        nc.sync.dma_start(out=page[2][:], in_=page_rows[2])
+        nc.sync.dma_start(idx3[:], offs3)
+        nc.sync.dma_start(out=page[3][:], in_=page_rows[3])
+        nc.sync.dma_start(out=w3_raw[:], in_=w3.rearrange("(p j) n -> p j n", j=PACK))
+        with nc.allow_non_contiguous_dma(reason="one gain for each output row, rows lie on the partitions"):
+            nc.sync.dma_start(out=gains[:], in_=gain.rearrange("(j p) -> p j", p=P))
+
+        v_w = [held.tile([P, S], U32, name="v_w%d" % a, align_bytes=64) for a in range(PASSES)]
+        v_sc_packed = held.tile([P, S], U8, name="v_sc_packed", align_bytes=64)
+        wk_w = held.tile([P, PASSES, 2 * H], U8, name="wk_w", align_bytes=64)
+        wk_sc = held.tile([P, PASSES, H], U8, name="wk_sc", align_bytes=64)
+
+        def gather_words(a, lo, hi):
+            nc.vector.tensor_copy(
+                out=v_w[a][:, lo:hi], in_=tab_w[a][:].bitcast(U32).indirect(idx[:, lo // 16 : hi // 16])
+            )
+
+        gather_words(0, 0, S)
+        nc.vector.tensor_copy(out=v_sc_packed[:], in_=tab_sc[:].indirect(idx[:]))
+        for a in range(1, PASSES):
+            nc.scalar.dma_start(
+                out=v_sc_moved[a - 1][0:PLANE_ROWS, :].bitcast(I32),
+                in_=v_sc_packed[4 * a : 4 * a + PLANE_ROWS, :].bitcast(I32),
+            )
+        v_sc = [v_sc_packed] + v_sc_moved
+        nc.vector.tensor_copy(
+            out=wk_w[:].bitcast(U16).rearrange("p a (t m) -> p a t m", t=PACK),
+            in_=wk_raw[:].bitcast(U16).rearrange("p a (m t) -> p a t m", t=PACK),
+        )
+        gather_words(1, 0, S)
+        nc.vector.tensor_copy(
+            out=wk_sc[:].rearrange("p a (t m) -> p a t m", t=PACK),
+            in_=wk_sc_raw[:].rearrange("p a (m t) -> p a t m", t=PACK),
+        )
+        for h in range(HALVES):
+            gather_words(2, h * BANK, (h + 1) * BANK)
+
+        wn_codes = held.tile([P, PASSES, H], U32, name="wn_codes", align_bytes=64)
+        wn_sc = held.tile([P, PASSES, H], U8, name="wn_sc", align_bytes=64)
+
+        def quantise_wn(a, t_lo, t_hi):
+            width = (t_hi - t_lo) * P
+            grouped = held.tile([P, width * PACK], BF16, name="wn_grouped%d_%d" % (a, t_lo), align_bytes=64)
+            nc.scalar.copy(
+                out=grouped[:].rearrange("p (t m j) -> p m j t", m=P, j=PACK),
+                in_=wn_raw[a][:].rearrange("p j (m t) -> p m j t", t=PACK)[:, :, :, t_lo:t_hi],
+            )
+            cols = slice(t_lo * P, t_hi * P)
+            nc.vector.quantize_mx(out=wn_codes[:, a, cols].bitcast(FP8X4), scales=wn_sc[:, a, cols], in_=grouped[:])
+
+        keep = [held.tile([P, S], F32, name="keep%d" % t, align_bytes=64) for t in range(PACK)]
+
+        def bank(i):
+            return psum.tile([P, BANK], F32, name="acc", tag="bank%d" % (i % 8))
+
+        keep_pair = (0, 2, 1, 3)
+        fresh_pair = (1, 3, 0, 2)
+
+        def make_keep(t):
+            for h in range(HALVES):
+                cols = slice(h * BANK, (h + 1) * BANK)
+                acc = bank(2 * keep_pair[t] + h)
+                for a in range(PASSES):
+                    nc.tensor.matmul_mx(
+                        out=acc[:],
+                        lhsT=wk_w[:, a, 2 * P * t : 2 * P * (t + 1)].bitcast(FP4X4),
+                        lhsT_scale=wk_sc[:, a, P * t : P * (t + 1)],
+                        rhs=v_w[a][:, cols].bitcast(FP8X4),
+                        rhs_scale=v_sc[a][:, cols],
+                        start=(a == 0),
+                        stop=(a == PASSES - 1),
+                    )
+                nc.scalar.activation(out=keep[t][:, cols], in_=acc[:], func=ACT.Sigmoid, bias=bias[:, t : t + 1])
+
+        def make_fresh(t):
+            banks = []
+            for h in range(HALVES):
+                cols = slice(h * BANK, (h + 1) * BANK)
+                acc = bank(2 * fresh_pair[t] + h)
+                for a in range(PASSES):
+                    nc.tensor.matmul_mx(
+                        out=acc[:],
+                        lhsT=wn_codes[:, a, P * t : P * (t + 1)].bitcast(FP8X4),
+                        lhsT_scale=wn_sc[:, a, P * t : P * (t + 1)],
+                        rhs=v_w[a][:, cols].bitcast(FP8X4),
+                        rhs_scale=v_sc[a][:, cols],
+                        start=(a == 0),
+                        stop=(a == PASSES - 1),
+                    )
+                banks.append(acc)
+            return banks
+
+        def fetch_damped(t):
+            damped = ring.tile([P, S], F32, name="damped", align_bytes=64)
+            nc.vector.tensor_tensor(out=damped[:], in0=page[t][:].indirect(idx2[:]), in1=keep[t][:], op=ALU.mult)
+            return damped
+
+        def revise(damped, banks):
+            revised = ring.tile([P, S], F32, name="revised", align_bytes=64)
+            for h in range(HALVES):
+                cols = slice(h * BANK, (h + 1) * BANK)
+                nc.vector.tensor_tensor(out=revised[:, cols], in0=banks[h][:], in1=damped[:, cols], op=ALU.max)
+            return revised
+
+        quantise_wn(0, 0, PACK)
+        make_keep(0)
+        quantise_wn(1, 0, PACK)
+        damped = fetch_damped(0)
+        quantise_wn(2, 0, 1)
+        fresh = make_fresh(0)
+        quantise_wn(2, 1, PACK)
+        for t in range(PACK):
+            revised = revise(damped, fresh)
+            if t + 1 < PACK:
+                make_keep(t + 1)
+                fresh = make_fresh(t + 1)
+                damped = fetch_damped(t + 1)
+            nc.vector.tensor_copy(out=page[t][:].indirect(idx2[:]), in_=revised[:])
+
+        w3_grouped = held.tile([P, N, PACK], BF16, name="w3_grouped", align_bytes=64)
+        nc.scalar.copy(
+            out=w3_grouped[:].rearrange("p (c i) t -> p c t i", i=4),
+            in_=w3_raw[:].rearrange("p t (c i) -> p c t i", i=4),
+        )
+        w3_codes = held.tile([P, N], U32, name="w3_codes", align_bytes=64)
+        w3_sc = held.tile([P, N], U8, name="w3_sc", align_bytes=64)
+        for lo, hi in ((0, 512), (512, N)):
+            nc.vector.quantize_mx(
+                out=w3_codes[:, lo:hi].bitcast(FP8X4),
+                scales=w3_sc[:, lo:hi],
+                in_=w3_grouped[:, lo:hi, :].rearrange("p n t -> p (n t)"),
+            )
+
+        out_rows = out.rearrange("(j p) m -> p j m", p=P)
+        starts = [sum(CHUNKS[:c]) for c in range(len(CHUNKS))]
+
+        def look_up(c):
+            lo, width = starts[c], CHUNKS[c]
+            picked = ring.tile([P, PACK, width], BF16, name="picked", align_bytes=64)
+            for t in range(PACK):
+                nc.vector.tensor_copy(
+                    out=picked[:, t, :], in_=page[t][:].indirect(idx3[:, lo // 16 : (lo + width) // 16])
+                )
+            grouped = ring.tile([P, width, PACK], BF16, name="x_grouped", align_bytes=64)
+            nc.scalar.copy(
+                out=grouped[:].rearrange("p (c i) t -> p c t i", i=4),
+                in_=picked[:].rearrange("p t (c i) -> p c t i", i=4),
+            )
+            return grouped
+
+        def multiply(c, grouped):
+            width = CHUNKS[c]
+            codes = ring.tile([P, width], U32, name="x_codes", align_bytes=64)
+            scales = ring.tile([P, width], U8, name="x_sc", align_bytes=64)
+            nc.vector.quantize_mx(
+                out=codes[:].bitcast(FP8X4), scales=scales[:], in_=grouped[:].rearrange("p m t -> p (m t)")
+            )
+            squashed = ring.tile([P, N_TILES, width], F32, name="squashed", align_bytes=64)
+            per_bank = min(BANK // width, N_TILES)
+            for j0 in range(0, N_TILES, per_bank):
+                count = min(per_bank, N_TILES - j0)
+                acc = bank(3 * c + j0 // per_bank)
+                for i in range(count):
+                    j = j0 + i
+                    nc.tensor.matmul_mx(
+                        out=acc[:, i * width : (i + 1) * width],
+                        lhsT=w3_codes[:, j * P : (j + 1) * P].bitcast(FP8X4),
+                        lhsT_scale=w3_sc[:, j * P : (j + 1) * P],
+                        rhs=codes[:].bitcast(FP8X4),
+                        rhs_scale=scales[:],
+                        start=True,
+                        stop=True,
+                    )
+                nc.scalar.activation(
+                    out=squashed[:, j0 : j0 + count, :].rearrange("p j m -> p (j m)"),
+                    in_=acc[:, : count * width],
+                    func=ACT.Tanh,
+                )
+            return squashed
+
+        def finish(c, squashed):
+            lo, width = starts[c], CHUNKS[c]
+            result = ring.tile([P, N_TILES, width], F32, name="result", align_bytes=64)
+            for j0 in range(0, N_TILES, 2):
+                for j in (j0, j0 + 1):
+                    nc.vector.tensor_scalar(
+                        out=result[:, j, :],
+                        in0=squashed[:, j, :],
+                        scalar1=gains[:, j : j + 1],
+                        scalar2=None,
+                        op0=ALU.mult,
+                    )
+                nc.sync.dma_start(out=out_rows[:, j0 : j0 + 2, lo : lo + width], in_=result[:, j0 : j0 + 2, :])
+
+        grouped = {}
+        squashed = {}
+        for step in range(len(CHUNKS) + 2):
+            if step < len(CHUNKS):
+                grouped[step] = look_up(step)
+            if 0 <= step - 1 < len(CHUNKS):
+                squashed[step - 1] = multiply(step - 1, grouped[step - 1])
+            if 0 <= step - 2 < len(CHUNKS):
+                finish(step - 2, squashed[step - 2])

@@ -40,60 +40,62 @@ def tile_list_hinge_history_update_kernel(
         idx2 = lists.tile([P, S // 16], U16, name="idx2")
         idx3 = lists.tile([P, P3 // 16], U16, name="idx3")
 
+        def staged(slot, name, shape, dtype):
+            return held.tile(shape, dtype, name=name, tag=slot, align_bytes=64)
+
         tab_sc = held.tile([P, T], U8, name="tab_sc", align_bytes=64)
-        wk_sc_raw = held.tile([P, PASSES, H], U8, name="wk_sc_raw", align_bytes=64)
+        wk_sc_raw = staged("wk_scales_then_v1", "wk_sc_raw", [P, PASSES, H], U8)
         v_sc_moved = [held.tile([P, S], U8, name="v_sc_moved%d" % a, align_bytes=64) for a in range(1, PASSES)]
-        nc.vector.memset(tab_sc[:].bitcast(I32), 0)
-        nc.vector.memset(wk_sc_raw[:].rearrange("p a n -> p (a n)").bitcast(I32), 0)
+        nc.gpsimd.memset(tab_sc[:].bitcast(I32), 0)
+        nc.gpsimd.memset(wk_sc_raw[:].rearrange("p a n -> p (a n)").bitcast(I32), 0)
         for moved in v_sc_moved:
             nc.vector.memset(moved[:].bitcast(I32), 0)
 
-        for q in range(4):
-            nc.scalar.dma_start(
-                out=tab_sc[32 * q : 32 * q + 4 * PASSES, :].bitcast(I32),
-                in_=tab_scales[:, 4 * q : 4 * q + 4, :].bitcast(I32),
-            )
-        for q in range(4):
-            nc.gpsimd.dma_start(
-                out=wk_sc_raw[32 * q : 32 * q + 4, :, :].bitcast(I32),
-                in_=wk_scales[:, 4 * q : 4 * q + 4, :].rearrange("a r n -> r a n").bitcast(I32),
-            )
         bias = held.tile([P, PACK], F32, name="bias")
         nc.gpsimd.dma_start(out=bias[:], in_=bk.rearrange("(p t) -> p t", t=PACK))
         gains = held.tile([P, N_TILES], F32, name="gains")
+        with nc.allow_non_contiguous_dma(reason="one gain for each output row, rows lie on the partitions"):
+            nc.gpsimd.dma_start(out=gains[:], in_=gain.rearrange("(j p) -> p j", p=P))
 
         tab_w = [held.tile([P, T], I32, name="tab_w%d" % a, align_bytes=64) for a in range(PASSES)]
         wk_raw = held.tile([P, PASSES, H // 2], I32, name="wk_raw", align_bytes=64)
         page = [held.tile([P, T2], F32, name="page%d" % t, align_bytes=64) for t in range(PACK)]
-        wn_raw = [held.tile([P, PACK, H], F32, name="wn_raw%d" % a, align_bytes=64) for a in range(PASSES)]
+        wn_raw = [staged("wn_then_keep%d" % a, "wn_raw%d" % a, [P, PACK, H], F32) for a in range(PASSES)]
         w3_raw = held.tile([P, PACK, N], F32, name="w3_raw", align_bytes=64)
         page_rows = page0.rearrange("(p t) c -> t p c", t=PACK)
-
-        def load_table(a):
-            nc.sync.dma_start(out=tab_w[a][:], in_=tab_words[a].rearrange("p n i -> p (n i)").bitcast(I32))
 
         def load_wn(a):
             rows = wn[a * P * PACK : (a + 1) * P * PACK, :]
             nc.sync.dma_start(out=wn_raw[a][:], in_=rows.rearrange("(p j) c -> p j c", j=PACK))
 
         nc.sync.dma_start(idx[:], offs)
-        load_table(0)
+        tab_rows = tab_words.rearrange("a p n i -> p a (n i)").bitcast(I32)
+        nc.sync.dma_start(out=tab_w[0][:], in_=tab_rows[:, 0, :])
+        for q in range(4):
+            queue = nc.sync if q % 2 == 0 else nc.scalar
+            queue.dma_start(
+                out=tab_sc[32 * q : 32 * q + 4 * PASSES, :].bitcast(I32),
+                in_=tab_scales[:, 4 * q : 4 * q + 4, :].bitcast(I32),
+            )
         nc.sync.dma_start(out=wk_raw[:], in_=wk_words.rearrange("a p n -> p a n").bitcast(I32))
-        load_table(1)
-        load_table(2)
+        nc.sync.dma_start(out=tab_w[1][:], in_=tab_rows[:, 1, :])
+        load_wn(0)
+        for q in range(4):
+            nc.sync.dma_start(
+                out=wk_sc_raw[32 * q : 32 * q + 4, :, :].bitcast(I32),
+                in_=wk_scales[:, 4 * q : 4 * q + 4, :].rearrange("a r n -> r a n").bitcast(I32),
+            )
+        nc.sync.dma_start(out=tab_w[2][:], in_=tab_rows[:, 2, :])
         nc.sync.dma_start(idx2[:], offs2)
+        load_wn(1)
         nc.sync.dma_start(out=page[0][:], in_=page_rows[0])
-        for a in range(PASSES):
-            load_wn(a)
-        nc.sync.dma_start(out=page[1][:], in_=page_rows[1])
-        nc.sync.dma_start(out=page[2][:], in_=page_rows[2])
-        nc.sync.dma_start(idx3[:], offs3)
-        nc.sync.dma_start(out=page[3][:], in_=page_rows[3])
+        load_wn(2)
+        for t in range(1, PACK):
+            nc.sync.dma_start(out=page[t][:], in_=page_rows[t])
         nc.sync.dma_start(out=w3_raw[:], in_=w3.rearrange("(p j) n -> p j n", j=PACK))
-        with nc.allow_non_contiguous_dma(reason="one gain for each output row, rows lie on the partitions"):
-            nc.sync.dma_start(out=gains[:], in_=gain.rearrange("(j p) -> p j", p=P))
+        nc.sync.dma_start(idx3[:], offs3)
 
-        v_w = [held.tile([P, S], U32, name="v_w%d" % a, align_bytes=64) for a in range(PASSES)]
+        v_w = {a: held.tile([P, S], U32, name="v_w%d" % a, align_bytes=64) for a in (0, 2)}
         v_sc_packed = held.tile([P, S], U8, name="v_sc_packed", align_bytes=64)
         wk_w = held.tile([P, PASSES, 2 * H], U8, name="wk_w", align_bytes=64)
         wk_sc = held.tile([P, PASSES, H], U8, name="wk_sc", align_bytes=64)
@@ -115,11 +117,12 @@ def tile_list_hinge_history_update_kernel(
             out=wk_w[:].bitcast(U16).rearrange("p a (t m) -> p a t m", t=PACK),
             in_=wk_raw[:].bitcast(U16).rearrange("p a (m t) -> p a t m", t=PACK),
         )
-        gather_words(1, 0, S)
         nc.vector.tensor_copy(
             out=wk_sc[:].rearrange("p a (t m) -> p a t m", t=PACK),
             in_=wk_sc_raw[:].rearrange("p a (m t) -> p a t m", t=PACK),
         )
+        v_w[1] = staged("wk_scales_then_v1", "v_w1", [P, S], U32)
+        gather_words(1, 0, S)
         for h in range(HALVES):
             gather_words(2, h * BANK, (h + 1) * BANK)
 
@@ -136,15 +139,16 @@ def tile_list_hinge_history_update_kernel(
             cols = slice(t_lo * P, t_hi * P)
             nc.vector.quantize_mx(out=wn_codes[:, a, cols].bitcast(FP8X4), scales=wn_sc[:, a, cols], in_=grouped[:])
 
-        keep = [held.tile([P, S], F32, name="keep%d" % t, align_bytes=64) for t in range(PACK)]
+        keep = {}
 
         def bank(i):
             return psum.tile([P, BANK], F32, name="acc", tag="bank%d" % (i % 8))
 
-        keep_pair = (0, 2, 1, 3)
-        fresh_pair = (1, 3, 0, 2)
+        keep_pair = (0, 0, 1, 2)
+        fresh_pair = (1, 2, 3, 0)
 
         def make_keep(t):
+            keep[t] = staged("wn_then_keep%d" % ((t + 1) % PASSES), "keep%d" % t, [P, S], F32)
             for h in range(HALVES):
                 cols = slice(h * BANK, (h + 1) * BANK)
                 acc = bank(2 * keep_pair[t] + h)
@@ -178,9 +182,16 @@ def tile_list_hinge_history_update_kernel(
                 banks.append(acc)
             return banks
 
-        def fetch_damped(t):
-            damped = ring.tile([P, S], F32, name="damped", align_bytes=64)
-            nc.vector.tensor_tensor(out=damped[:], in0=page[t][:].indirect(idx2[:]), in1=keep[t][:], op=ALU.mult)
+        def fetch_damped(t, pieces):
+            damped = held.tile([P, S], F32, name="damped", align_bytes=64)
+            width = S // pieces
+            for lo in range(0, S, width):
+                nc.vector.tensor_tensor(
+                    out=damped[:, lo : lo + width],
+                    in0=page[t][:].indirect(idx2[:, lo // 16 : (lo + width) // 16]),
+                    in1=keep[t][:, lo : lo + width],
+                    op=ALU.mult,
+                )
             return damped
 
         def revise(damped, banks):
@@ -191,9 +202,9 @@ def tile_list_hinge_history_update_kernel(
             return revised
 
         quantise_wn(0, 0, PACK)
-        make_keep(0)
         quantise_wn(1, 0, PACK)
-        damped = fetch_damped(0)
+        make_keep(0)
+        damped = fetch_damped(0, HALVES)
         quantise_wn(2, 0, 1)
         fresh = make_fresh(0)
         quantise_wn(2, 1, PACK)
@@ -202,7 +213,7 @@ def tile_list_hinge_history_update_kernel(
             if t + 1 < PACK:
                 make_keep(t + 1)
                 fresh = make_fresh(t + 1)
-                damped = fetch_damped(t + 1)
+                damped = fetch_damped(t + 1, 1)
             nc.vector.tensor_copy(out=page[t][:].indirect(idx2[:]), in_=revised[:])
 
         w3_grouped = held.tile([P, N, PACK], BF16, name="w3_grouped", align_bytes=64)

@@ -44,7 +44,7 @@ def tile_list_hinge_history_update_kernel(
             return held.tile(shape, dtype, name=name, tag=slot, align_bytes=64)
 
         tab_sc = held.tile([P, T], U8, name="tab_sc", align_bytes=64)
-        wk_sc_raw = staged("wk_scales_then_v1", "wk_sc_raw", [P, PASSES, H], U8)
+        wk_sc_raw = staged("wk_scales_then_v2", "wk_sc_raw", [P, PASSES, H], U8)
         v_sc_moved = [held.tile([P, S], U8, name="v_sc_moved%d" % a, align_bytes=64) for a in range(1, PASSES)]
         nc.gpsimd.memset(tab_sc[:].bitcast(I32), 0)
         nc.gpsimd.memset(wk_sc_raw[:].rearrange("p a n -> p (a n)").bitcast(I32), 0)
@@ -68,6 +68,12 @@ def tile_list_hinge_history_update_kernel(
             rows = wn[a * P * PACK : (a + 1) * P * PACK, :]
             nc.sync.dma_start(out=wn_raw[a][:], in_=rows.rearrange("(p j) c -> p j c", j=PACK))
 
+        def load_wk_scales(q):
+            nc.sync.dma_start(
+                out=wk_sc_raw[32 * q : 32 * q + 4, :, :].bitcast(I32),
+                in_=wk_scales[:, 4 * q : 4 * q + 4, :].rearrange("a r n -> r a n").bitcast(I32),
+            )
+
         nc.sync.dma_start(idx[:], offs)
         tab_rows = tab_words.rearrange("a p n i -> p a (n i)").bitcast(I32)
         nc.sync.dma_start(out=tab_w[0][:], in_=tab_rows[:, 0, :])
@@ -80,22 +86,21 @@ def tile_list_hinge_history_update_kernel(
         nc.sync.dma_start(out=wk_raw[:], in_=wk_words.rearrange("a p n -> p a n").bitcast(I32))
         nc.sync.dma_start(out=tab_w[1][:], in_=tab_rows[:, 1, :])
         load_wn(0)
-        for q in range(4):
-            nc.sync.dma_start(
-                out=wk_sc_raw[32 * q : 32 * q + 4, :, :].bitcast(I32),
-                in_=wk_scales[:, 4 * q : 4 * q + 4, :].rearrange("a r n -> r a n").bitcast(I32),
-            )
+        load_wk_scales(0)
+        load_wk_scales(1)
         nc.sync.dma_start(out=tab_w[2][:], in_=tab_rows[:, 2, :])
-        nc.sync.dma_start(idx2[:], offs2)
+        load_wk_scales(2)
+        load_wk_scales(3)
         load_wn(1)
         nc.sync.dma_start(out=page[0][:], in_=page_rows[0])
+        nc.sync.dma_start(idx2[:], offs2)
         load_wn(2)
         for t in range(1, PACK):
             nc.sync.dma_start(out=page[t][:], in_=page_rows[t])
         nc.sync.dma_start(out=w3_raw[:], in_=w3.rearrange("(p j) n -> p j n", j=PACK))
         nc.sync.dma_start(idx3[:], offs3)
 
-        v_w = {a: held.tile([P, S], U32, name="v_w%d" % a, align_bytes=64) for a in (0, 2)}
+        v_w = {a: held.tile([P, S], U32, name="v_w%d" % a, align_bytes=64) for a in (0, 1)}
         v_sc_packed = held.tile([P, S], U8, name="v_sc_packed", align_bytes=64)
         wk_w = held.tile([P, PASSES, 2 * H], U8, name="wk_w", align_bytes=64)
         wk_sc = held.tile([P, PASSES, H], U8, name="wk_sc", align_bytes=64)
@@ -117,12 +122,12 @@ def tile_list_hinge_history_update_kernel(
             out=wk_w[:].bitcast(U16).rearrange("p a (t m) -> p a t m", t=PACK),
             in_=wk_raw[:].bitcast(U16).rearrange("p a (m t) -> p a t m", t=PACK),
         )
+        gather_words(1, 0, S)
         nc.vector.tensor_copy(
             out=wk_sc[:].rearrange("p a (t m) -> p a t m", t=PACK),
             in_=wk_sc_raw[:].rearrange("p a (m t) -> p a t m", t=PACK),
         )
-        v_w[1] = staged("wk_scales_then_v1", "v_w1", [P, S], U32)
-        gather_words(1, 0, S)
+        v_w[2] = staged("wk_scales_then_v2", "v_w2", [P, S], U32)
         for h in range(HALVES):
             gather_words(2, h * BANK, (h + 1) * BANK)
 

from contextlib import ExitStack

import concourse.mybir as mybir

K, H, N, T, S, T2, P3 = 1536, 512, 768, 2048, 1024, 2048, 1024
FLOPS = 2 * (2 * K * H * S + H * N * P3)

F32 = mybir.dt.float32
BF16 = mybir.dt.bfloat16
I32 = mybir.dt.int32
U32 = mybir.dt.uint32
U16 = mybir.dt.uint16
U8 = mybir.dt.uint8
FP8X4 = mybir.dt.float8_e4m3fn_x4
FP4X4 = mybir.dt.float4_e2m1fn_x4
ACT = mybir.ActivationFunctionType
ALU = mybir.AluOpType

P = 128
PACK = 4
PASSES = K // (P * PACK)
BANK = 512
HALVES = S // BANK
N_TILES = N // P
CHUNKS = (256, 256, 256, 256)
PLANE_ROWS = 100


def tile_list_hinge_history_update_kernel(
    tc, tab_words, tab_scales, offs, offs2, offs3, wk_words, wk_scales, bk, wn, page0, w3, gain, out
):
    nc = tc.nc
    with ExitStack() as ctx:
        lists = ctx.enter_context(tc.tile_pool(name="lists", bufs=1))
        held = ctx.enter_context(tc.tile_pool(name="held", bufs=1))
        ring = ctx.enter_context(tc.tile_pool(name="ring", bufs=2))
        psum = ctx.enter_context(tc.psum_pool(name="psum", bufs=1))

        idx = lists.tile([P, S // 16], U16, name="idx")
        idx2 = lists.tile([P, S // 16], U16, name="idx2")
        idx3 = lists.tile([P, P3 // 16], U16, name="idx3")

        def staged(slot, name, shape, dtype):
            return held.tile(shape, dtype, name=name, tag=slot, align_bytes=64)

        tab_sc = held.tile([P, T], U8, name="tab_sc", align_bytes=64)
        wk_sc_raw = staged("wk_scales_then_v2", "wk_sc_raw", [P, PASSES, H], U8)
        v_sc_moved = [held.tile([P, S], U8, name="v_sc_moved%d" % a, align_bytes=64) for a in range(1, PASSES)]
        nc.gpsimd.memset(tab_sc[:].bitcast(I32), 0)
        nc.gpsimd.memset(wk_sc_raw[:].rearrange("p a n -> p (a n)").bitcast(I32), 0)
        for moved in v_sc_moved:
            nc.vector.memset(moved[:].bitcast(I32), 0)

        bias = held.tile([P, PACK], F32, name="bias")
        nc.gpsimd.dma_start(out=bias[:], in_=bk.rearrange("(p t) -> p t", t=PACK))
        gains = held.tile([P, N_TILES], F32, name="gains")
        with nc.allow_non_contiguous_dma(reason="one gain for each output row, rows lie on the partitions"):
            nc.gpsimd.dma_start(out=gains[:], in_=gain.rearrange("(j p) -> p j", p=P))

        tab_w = [held.tile([P, T], I32, name="tab_w%d" % a, align_bytes=64) for a in range(PASSES)]
        wk_raw = held.tile([P, PASSES, H // 2], I32, name="wk_raw", align_bytes=64)
        page = [held.tile([P, T2], F32, name="page%d" % t, align_bytes=64) for t in range(PACK)]
        wn_raw = [staged("wn_then_keep%d" % a, "wn_raw%d" % a, [P, PACK, H], F32) for a in range(PASSES)]
        w3_raw = held.tile([P, PACK, N], F32, name="w3_raw", align_bytes=64)
        page_rows = page0.rearrange("(p t) c -> t p c", t=PACK)

        def load_wn(a):
            rows = wn[a * P * PACK : (a + 1) * P * PACK, :]
            nc.sync.dma_start(out=wn_raw[a][:], in_=rows.rearrange("(p j) c -> p j c", j=PACK))

        def load_wk_scales(q):
            nc.sync.dma_start(
                out=wk_sc_raw[32 * q : 32 * q + 4, :, :].bitcast(I32),
                in_=wk_scales[:, 4 * q : 4 * q + 4, :].rearrange("a r n -> r a n").bitcast(I32),
            )

        nc.sync.dma_start(idx[:], offs)
        tab_rows = tab_words.rearrange("a p n i -> p a (n i)").bitcast(I32)
        nc.sync.dma_start(out=tab_w[0][:], in_=tab_rows[:, 0, :])
        for q in range(4):
            queue = nc.sync if q % 2 == 0 else nc.scalar
            queue.dma_start(
                out=tab_sc[32 * q : 32 * q + 4 * PASSES, :].bitcast(I32),
                in_=tab_scales[:, 4 * q : 4 * q + 4, :].bitcast(I32),
            )
        nc.sync.dma_start(out=wk_raw[:], in_=wk_words.rearrange("a p n -> p a n").bitcast(I32))
        nc.sync.dma_start(out=tab_w[1][:], in_=tab_rows[:, 1, :])
        load_wn(0)
        load_wk_scales(0)
        load_wk_scales(1)
        nc.sync.dma_start(out=tab_w[2][:], in_=tab_rows[:, 2, :])
        load_wk_scales(2)
        load_wk_scales(3)
        load_wn(1)
        nc.sync.dma_start(out=page[0][:], in_=page_rows[0])
        nc.sync.dma_start(idx2[:], offs2)
        load_wn(2)
        for t in range(1, PACK):
            nc.sync.dma_start(out=page[t][:], in_=page_rows[t])
        nc.sync.dma_start(out=w3_raw[:], in_=w3.rearrange("(p j) n -> p j n", j=PACK))
        nc.sync.dma_start(idx3[:], offs3)

        v_w = {a: held.tile([P, S], U32, name="v_w%d" % a, align_bytes=64) for a in (0, 1)}
        v_sc_packed = held.tile([P, S], U8, name="v_sc_packed", align_bytes=64)
        wk_w = held.tile([P, PASSES, 2 * H], U8, name="wk_w", align_bytes=64)
        wk_sc = held.tile([P, PASSES, H], U8, name="wk_sc", align_bytes=64)

        def gather_words(a, lo, hi):
            nc.vector.tensor_copy(
                out=v_w[a][:, lo:hi], in_=tab_w[a][:].bitcast(U32).indirect(idx[:, lo // 16 : hi // 16])
            )

        gather_words(0, 0, S)
        nc.vector.tensor_copy(out=v_sc_packed[:], in_=tab_sc[:].indirect(idx[:]))
        for a in range(1, PASSES):
            nc.scalar.dma_start(
                out=v_sc_moved[a - 1][0:PLANE_ROWS, :].bitcast(I32),
                in_=v_sc_packed[4 * a : 4 * a + PLANE_ROWS, :].bitcast(I32),
            )
        v_sc = [v_sc_packed] + v_sc_moved
        nc.vector.tensor_copy(
            out=wk_w[:].bitcast(U16).rearrange("p a (t m) -> p a t m", t=PACK),
            in_=wk_raw[:].bitcast(U16).rearrange("p a (m t) -> p a t m", t=PACK),
        )
        gather_words(1, 0, S)
        nc.vector.tensor_copy(
            out=wk_sc[:].rearrange("p a (t m) -> p a t m", t=PACK),
            in_=wk_sc_raw[:].rearrange("p a (m t) -> p a t m", t=PACK),
        )
        v_w[2] = staged("wk_scales_then_v2", "v_w2", [P, S], U32)
        for h in range(HALVES):
            gather_words(2, h * BANK, (h + 1) * BANK)

        wn_codes = held.tile([P, PASSES, H], U32, name="wn_codes", align_bytes=64)
        wn_sc = held.tile([P, PASSES, H], U8, name="wn_sc", align_bytes=64)

        def quantise_wn(a, t_lo, t_hi):
            width = (t_hi - t_lo) * P
            grouped = held.tile([P, width * PACK], BF16, name="wn_grouped%d_%d" % (a, t_lo), align_bytes=64)
            nc.scalar.copy(
                out=grouped[:].rearrange("p (t m j) -> p m j t", m=P, j=PACK),
                in_=wn_raw[a][:].rearrange("p j (m t) -> p m j t", t=PACK)[:, :, :, t_lo:t_hi],
            )
            cols = slice(t_lo * P, t_hi * P)
            nc.vector.quantize_mx(out=wn_codes[:, a, cols].bitcast(FP8X4), scales=wn_sc[:, a, cols], in_=grouped[:])

        keep = {}

        def bank(i):
            return psum.tile([P, BANK], F32, name="acc", tag="bank%d" % (i % 8))

        keep_pair = (0, 0, 1, 2)
        fresh_pair = (1, 2, 3, 0)

        def make_keep(t):
            keep[t] = staged("wn_then_keep%d" % ((t + 1) % PASSES), "keep%d" % t, [P, S], F32)
            for h in range(HALVES):
                cols = slice(h * BANK, (h + 1) * BANK)
                acc = bank(2 * keep_pair[t] + h)
                for a in range(PASSES):
                    nc.tensor.matmul_mx(
                        out=acc[:],
                        lhsT=wk_w[:, a, 2 * P * t : 2 * P * (t + 1)].bitcast(FP4X4),
                        lhsT_scale=wk_sc[:, a, P * t : P * (t + 1)],
                        rhs=v_w[a][:, cols].bitcast(FP8X4),
                        rhs_scale=v_sc[a][:, cols],
                        start=(a == 0),
                        stop=(a == PASSES - 1),
                    )
                nc.scalar.activation(out=keep[t][:, cols], in_=acc[:], func=ACT.Sigmoid, bias=bias[:, t : t + 1])

        def make_fresh(t):
            banks = []
            for h in range(HALVES):
                cols = slice(h * BANK, (h + 1) * BANK)
                acc = bank(2 * fresh_pair[t] + h)
                for a in range(PASSES):
                    nc.tensor.matmul_mx(
                        out=acc[:],
                        lhsT=wn_codes[:, a, P * t : P * (t + 1)].bitcast(FP8X4),
                        lhsT_scale=wn_sc[:, a, P * t : P * (t + 1)],
                        rhs=v_w[a][:, cols].bitcast(FP8X4),
                        rhs_scale=v_sc[a][:, cols],
                        start=(a == 0),
                        stop=(a == PASSES - 1),
                    )
                banks.append(acc)
            return banks

        def fetch_damped(t, pieces):
            damped = held.tile([P, S], F32, name="damped", align_bytes=64)
            width = S // pieces
            for lo in range(0, S, width):
                nc.vector.tensor_tensor(
                    out=damped[:, lo : lo + width],
                    in0=page[t][:].indirect(idx2[:, lo // 16 : (lo + width) // 16]),
                    in1=keep[t][:, lo : lo + width],
                    op=ALU.mult,
                )
            return damped

        def revise(damped, banks):
            revised = ring.tile([P, S], F32, name="revised", align_bytes=64)
            for h in range(HALVES):
                cols = slice(h * BANK, (h + 1) * BANK)
                nc.vector.tensor_tensor(out=revised[:, cols], in0=banks[h][:], in1=damped[:, cols], op=ALU.max)
            return revised

        quantise_wn(0, 0, PACK)
        quantise_wn(1, 0, PACK)
        make_keep(0)
        damped = fetch_damped(0, HALVES)
        quantise_wn(2, 0, 1)
        fresh = make_fresh(0)
        quantise_wn(2, 1, PACK)
        for t in range(PACK):
            revised = revise(damped, fresh)
            if t + 1 < PACK:
                make_keep(t + 1)
                fresh = make_fresh(t + 1)
                damped = fetch_damped(t + 1, 1)
            nc.vector.tensor_copy(out=page[t][:].indirect(idx2[:]), in_=revised[:])

        w3_grouped = held.tile([P, N, PACK], BF16, name="w3_grouped", align_bytes=64)
        nc.scalar.copy(
            out=w3_grouped[:].rearrange("p (c i) t -> p c t i", i=4),
            in_=w3_raw[:].rearrange("p t (c i) -> p c t i", i=4),
        )
        w3_codes = held.tile([P, N], U32, name="w3_codes", align_bytes=64)
        w3_sc = held.tile([P, N], U8, name="w3_sc", align_bytes=64)
        for lo, hi in ((0, 512), (512, N)):
            nc.vector.quantize_mx(
                out=w3_codes[:, lo:hi].bitcast(FP8X4),
                scales=w3_sc[:, lo:hi],
                in_=w3_grouped[:, lo:hi, :].rearrange("p n t -> p (n t)"),
            )

        out_rows = out.rearrange("(j p) m -> p j m", p=P)
        starts = [sum(CHUNKS[:c]) for c in range(len(CHUNKS))]

        def look_up(c):
            lo, width = starts[c], CHUNKS[c]
            picked = ring.tile([P, PACK, width], BF16, name="picked", align_bytes=64)
            for t in range(PACK):
                nc.vector.tensor_copy(
                    out=picked[:, t, :], in_=page[t][:].indirect(idx3[:, lo // 16 : (lo + width) // 16])
                )
            grouped = ring.tile([P, width, PACK], BF16, name="x_grouped", align_bytes=64)
            nc.scalar.copy(
                out=grouped[:].rearrange("p (c i) t -> p c t i", i=4),
                in_=picked[:].rearrange("p t (c i) -> p c t i", i=4),
            )
            return grouped

        def multiply(c, grouped):
            width = CHUNKS[c]
            codes = ring.tile([P, width], U32, name="x_codes", align_bytes=64)
            scales = ring.tile([P, width], U8, name="x_sc", align_bytes=64)
            nc.vector.quantize_mx(
                out=codes[:].bitcast(FP8X4), scales=scales[:], in_=grouped[:].rearrange("p m t -> p (m t)")
            )
            squashed = ring.tile([P, N_TILES, width], F32, name="squashed", align_bytes=64)
            per_bank = min(BANK // width, N_TILES)
            for j0 in range(0, N_TILES, per_bank):
                count = min(per_bank, N_TILES - j0)
                acc = bank(3 * c + j0 // per_bank)
                for i in range(count):
                    j = j0 + i
                    nc.tensor.matmul_mx(
                        out=acc[:, i * width : (i + 1) * width],
                        lhsT=w3_codes[:, j * P : (j + 1) * P].bitcast(FP8X4),
                        lhsT_scale=w3_sc[:, j * P : (j + 1) * P],
                        rhs=codes[:].bitcast(FP8X4),
                        rhs_scale=scales[:],
                        start=True,
                        stop=True,
                    )
                nc.scalar.activation(
                    out=squashed[:, j0 : j0 + count, :].rearrange("p j m -> p (j m)"),
                    in_=acc[:, : count * width],
                    func=ACT.Tanh,
                )
            return squashed

        def finish(c, squashed):
            lo, width = starts[c], CHUNKS[c]
            result = ring.tile([P, N_TILES, width], F32, name="result", align_bytes=64)
            for j0 in range(0, N_TILES, 2):
                for j in (j0, j0 + 1):
                    nc.vector.tensor_scalar(
                        out=result[:, j, :],
                        in0=squashed[:, j, :],
                        scalar1=gains[:, j : j + 1],
                        scalar2=None,
                        op0=ALU.mult,
                    )
                nc.sync.dma_start(out=out_rows[:, j0 : j0 + 2, lo : lo + width], in_=result[:, j0 : j0 + 2, :])

        grouped = {}
        squashed = {}
        for step in range(len(CHUNKS) + 2):
            if step < len(CHUNKS):
                grouped[step] = look_up(step)
            if 0 <= step - 1 < len(CHUNKS):
                squashed[step - 1] = multiply(step - 1, grouped[step - 1])
            if 0 <= step - 2 < len(CHUNKS):
                finish(step - 2, squashed[step - 2])
